import numpy as np
import ml_dtypes


def mxq(x, axis, fmt="e4m3"):
    dtype, down = {"e4m3": (ml_dtypes.float8_e4m3fn, 7), "e5m2": (ml_dtypes.float8_e5m2, 14)}[fmt]
    v = np.moveaxis(np.asarray(x, np.float32).astype(ml_dtypes.bfloat16).astype(np.float64), axis, -1)
    blocks = v.reshape(v.shape[:-1] + (-1, 32))
    amax = np.abs(blocks).max(-1, keepdims=True)
    byte = np.maximum(np.where(amax > 0, np.frexp(amax)[1] - 1 + 127, 0) - down, 1)
    scale = np.exp2(byte - 127.0)
    codes = (blocks / scale).astype(np.float32).astype(dtype).astype(np.float64)
    return np.moveaxis((codes * scale).reshape(v.shape), -1, axis)


WIDE = False


def mx_kscale(k):
    if not WIDE:
        return np.ones(k)
    levels = np.array([10, -10, 5, -5, 0])
    if k % 512:
        return np.exp2(np.random.permutation(np.resize(levels, k // 32))).repeat(32)
    a = np.empty((k // 512, 16))
    for p in range(k // 512):
        a[p, :8] = np.random.permutation(np.resize(levels, 8))
        for g in range(8):
            far = levels[np.abs(levels - a[p, g]) >= 10]
            a[p, g + 8] = far[np.random.randint(len(far))]
    return np.exp2(a.ravel()).repeat(32)


BF16 = ml_dtypes.bfloat16


def bf(x):
    return np.asarray(x, np.float32).astype(BF16)


def f64(x):
    return np.asarray(x).astype(np.float64)


E2M1 = np.array([0.0, 0.5, 1.0, 1.5, 2.0, 3.0, 4.0, 6.0, -0.0, -0.5, -1.0, -1.5, -2.0, -3.0, -4.0, -6.0])


def pack_weight(w, fmt):
    k, n = w.shape
    w = f64(bf(w)).reshape(k // 32, 32, n)
    amax = np.abs(w).max(1)
    if fmt == "e4m3":
        byte = np.frexp(amax)[1] - 1 + 127 - 7
    else:
        mant, ex = np.frexp(amax / 6.0)
        byte = np.where(mant > 0.5, ex, ex - 1) + 127
    byte = np.clip(np.where(amax > 0, byte, 1), 1, 254)
    scaled = (w * np.exp2(127.0 - byte)[:, None, :]).reshape(k, n).astype(np.float32)
    by_word = np.ascontiguousarray(scaled.reshape(k // 512, 128, 4, n).transpose(0, 1, 3, 2))
    if fmt == "e4m3":
        words = by_word.astype(ml_dtypes.float8_e4m3fn).view(np.uint8)
    else:
        c = by_word.astype(ml_dtypes.float4_e2m1fn).view(np.uint8) & 0xF
        words = c[..., 0::2] | (c[..., 1::2] << 4)
    return np.ascontiguousarray(words), np.ascontiguousarray(byte.astype(np.uint8).reshape(k // 512, 16, n))


def unpack_weight(words, scales, fmt):
    g, p, n, _ = words.shape
    if fmt == "e4m3":
        vals = np.ascontiguousarray(words).view(ml_dtypes.float8_e4m3fn).astype(np.float64)
    else:
        nib = np.empty((g, p, n, 4), np.uint8)
        nib[..., 0::2] = words & 0xF
        nib[..., 1::2] = words >> 4
        vals = E2M1[nib]
    vals = vals * np.repeat(np.exp2(scales.astype(np.float64) - 127.0), 8, axis=1)[..., None]
    return vals.transpose(0, 1, 3, 2).reshape(g * 512, n)
def pack4(w):
    words, scales = pack_weight(w, "e2m1")
    return words.reshape(words.shape[0], 128, -1), scales


def unpack4(words, scales):
    return unpack_weight(words.reshape(words.shape[0], 128, -1, 2), scales, "e2m1")


E4M3FN = np.array([(-1.0 if i & 128 else 1.0) * ((1.0 + (i & 7) / 8.0) * 2.0 ** (((i >> 3) & 15) - 7) if i & 120 else (i & 7) * 2.0 ** -9) for i in range(256)])


def e4m3fn_bytes(y):
    return np.clip(np.asarray(y, np.float64), -448.0, 448.0).astype(np.float32).astype(ml_dtypes.float8_e4m3fn).view(np.uint8)


def e4m3fn_values(b):
    return E4M3FN[b]


B, P, D, A, V = 1024, 512, 512, 512, 512


def draw0():
    s, t = mx_kscale(P), mx_kscale(D)
    h_prev = bf(np.random.standard_normal((B, P)) * s)
    q = bf(np.random.standard_normal((B, D)) * t)
    wg_words, wg_scales = pack4(np.random.standard_normal((P, D)) / np.sqrt(P) / s[:, None] * t)
    bg = bf(np.random.standard_normal(D) * 0.3 * t)
    wv_words, wv_scales = pack4(np.random.standard_normal((D, V)) / np.sqrt(D) / t[:, None])
    wk_words, wk_scales = pack4(np.random.standard_normal((D, A)) / np.sqrt(D) / t[:, None])
    wq_words, wq_scales = pack4(np.random.standard_normal((D, A)) / np.sqrt(D) / t[:, None])
    return {
        "h_prev": h_prev,
        "q": q,
        "wg_words": wg_words,
        "wg_scales": wg_scales,
        "bg": bg,
        "wv_words": wv_words,
        "wv_scales": wv_scales,
        "wk_words": wk_words,
        "wk_scales": wk_scales,
        "wq_words": wq_words,
        "wq_scales": wq_scales,
    }


def _project(u, wv, wk, wq):
    value = u @ wv
    k = u @ wk
    r = u @ wq
    return value, k, r


def _score(k, r):
    return np.sum(k * r, axis=-1) / np.sqrt(A)


def core(h_prev, q, wg_words, wg_scales, bg, wv_words, wv_scales, wk_words, wk_scales, wq_words, wq_scales):
    p = (mxq(f64(h_prev), 1, "e4m3") @ unpack4(wg_words, wg_scales)) + f64(bg)

    pm = mxq(p, 1, "e4m3")
    qm = mxq(f64(q), 1, "e4m3")
    wvm = unpack4(wv_words, wv_scales)
    wkm = unpack4(wk_words, wk_scales)
    wqm = unpack4(wq_words, wq_scales)

    vp, kp, rp = _project(pm, wvm, wkm, wqm)
    vq, kq, rq = _project(qm, wvm, wkm, wqm)

    sp = _score(kp, rp)
    sq = _score(kq, rq)

    logits = np.stack([sp, sq], axis=-1)
    e = np.exp(logits - logits.max(axis=-1, keepdims=True))
    weights = e / e.sum(axis=-1, keepdims=True)
    ap = weights[:, 0]
    aq = weights[:, 1]

    z = ap[:, None] * vp + aq[:, None] * vq
    return z


def setup_inputs():
    drawn = draw0()
    full = np.asarray(drawn['q']).astype(np.float64)
    scale = (np.abs(full).reshape(1024, 4, 128).max(axis=(2,)) / 448.0).astype(np.float32)
    given = {}
    for key, value in drawn.items():
        if key == 'q':
            given['q_bytes'] = e4m3fn_bytes(full / np.repeat(scale.astype(np.float64), 128, axis=1))
            given['q_scale'] = scale
        else:
            given[key] = value
    return given


def reference(h_prev, q_bytes, q_scale, wg_words, wg_scales, bg, wv_words, wv_scales, wk_words, wk_scales, wq_words, wq_scales):
    return core(h_prev, e4m3fn_values(q_bytes) * np.repeat(q_scale.astype(np.float64), 128, axis=1), wg_words, wg_scales, bg, wv_words, wv_scales, wk_words, wk_scales, wq_words, wq_scales)

import math
from contextlib import ExitStack

import concourse.mybir as mybir
from concourse.masks import make_identity

F32 = mybir.dt.float32
BF16 = mybir.dt.bfloat16
I32 = mybir.dt.int32
U32 = mybir.dt.uint32
U8 = mybir.dt.uint8
FP8 = mybir.dt.float8_e4m3fn
FP8X4 = mybir.dt.float8_e4m3fn_x4
FP4X4 = mybir.dt.float4_e2m1fn_x4
ACT = mybir.ActivationFunctionType
ALU = mybir.AluOpType

TOKENS, WIDTH = 1024, 512
P = 128
PACK = 4
TILES = TOKENS // P
PAIRS = TILES // 2
FLOPS = 7 * 2 * TOKENS * WIDTH * WIDTH
ORDER = "perm0 perm1 Th0 Th1 Eh0 Eh1 W2 W3 Qh0 W0 W1 Qh1 P0 P1 Tq0 Th2 Th3 P2 P3 Tq1 Pe0 Pe1 W4 Qp0 Eq0 Eh2 Eh3 W5 W6 Eq1 W7 Qq0 Qh2 Pe2 Pe3 Qh3 Qp1 P4 P5 Kp0 Tq2 P6 P7 Kq0 Tq3 Pe4 Pe5 Qq1 Qp2 Pe6 Pe7 Cp0 Eq2 Cq0 Eq3 Rp0 Kp1 Rq0 Kq1 Kp2 Rp1 Kq2 Rq1 Qq2 Qp3 Dp0 Qq3 Dq0 Cp1 Cq1 Cp2 G0 Cq2 Vp0 Kp3 Rp2 Kq3 Rq2 Dp1 Dq1 Dp2 Dq2 Sv0 Cp3 G1 Cq3 Vp1 Kp4 Rp3 Kq4 Rq3 Vp2 Vq0 Kp5 Dp3 Dq3 Z0 Sv1 Cp4 G2 Cq4 Sv2 Cp5 G3 Rp4 Kq5 Rq4 Vp3 Vq1 Kp6 Rp5 Kq6 Dp4 Dq4 Z1 Dp5 Cq5 Sv3 Cp6 G4 Cq6 Rq5 Vp4 Vq2 Kp7 Rp6 Kq7 Rq6 Vp5 Dq5 Z2 Dp6 Dq6 Sv4 Cp7 G5 Cq7 Sv5 G6 Vq3 Rp7 Rq7 Vp6 Vq4 Vp7 Vq5 Vq6 Z3 Dp7 Dq7 Z4 Z5 Sv6 G7 Sv7 Vq7 Z6 Z7".split()
WIDEN_ON_VECTOR = (0, 1, 4,)
MIX_ON_GPSIMD = ()


def tile_aitmadaptiveinformationtransfer_d1p_kernel(
    tc, h_prev, q_bytes, q_scale, wg_words, wg_scales, bg, wv_words, wv_scales, wk_words, wk_scales, wq_words, wq_scales, out
):
    nc = tc.nc
    h_rows = h_prev.rearrange("(p i) d -> p i d", i=TILES)
    q_rows = q_bytes.rearrange("(p i) d -> p (i d)", i=TILES)
    out_rows = out.rearrange("(p i) d -> p i d", i=TILES)

    with ExitStack() as ctx:
        keep = ctx.enter_context(tc.tile_pool(name="keep", bufs=1))
        psum = ctx.enter_context(tc.psum_pool(name="psum", bufs=1))
        ctx.enter_context(tc.manual_schedule())

        weight_codes, weight_plane = {}, {}
        for name in ("wg", "wk", "wq", "wv"):
            weight_codes[name] = keep.tile([P, 2 * WIDTH], U8, name=name + "_codes", align_bytes=64)
            weight_plane[name] = keep.tile([P, WIDTH], U8, name=name + "_plane", align_bytes=64)
            nc.vector.memset(weight_plane[name][:].bitcast(I32), 0)

        def load_words(name, words):
            nc.sync.dma_start(out=weight_codes[name][:].bitcast(I32), in_=words[0].bitcast(I32))

        def load_plane(name, scales, queue):
            for quad in range(4):
                queue.dma_start(
                    out=weight_plane[name][32 * quad : 32 * quad + 4, :].bitcast(I32),
                    in_=scales[0, 4 * quad : 4 * quad + 4, :].bitcast(I32),
                )

        q_raw, h_sb = {}, {}

        def load_q(half):
            q_raw[half] = keep.tile([P, 4 * WIDTH], U8, name="q_raw_%d" % half, align_bytes=64)
            nc.sync.dma_start(out=q_raw[half][:], in_=q_rows[:, 4 * WIDTH * half : 4 * WIDTH * (half + 1)])

        def load_h(j):
            h_sb[j] = keep.tile([P, 2, WIDTH], BF16, name="h_rows_%d" % j, align_bytes=64)
            nc.sync.dma_start(out=h_sb[j][:], in_=h_rows[:, 2 * j : 2 * j + 2, :])

        q_factor = keep.tile([P, TILES * 4], F32, name="q_factor")
        bias = keep.tile([P, PACK], BF16, name="bias")
        ident = keep.tile([P, P], F32, name="ident")
        warm = keep.tile([P, 1], F32, name="warm")
        warm_out = keep.tile([P, 1], F32, name="warm_out")
        load_h(0)
        load_words("wg", wg_words)
        load_plane("wg", wg_scales, nc.scalar)
        load_h(1)
        load_q(0)
        nc.vector.memset(warm[:], 0.0)
        nc.scalar.activation(out=warm_out[:], in_=warm[:], func=ACT.Sigmoid)
        make_identity(nc, ident[:])
        nc.gpsimd.dma_start(out=q_factor[:], in_=q_scale.rearrange("(p i) b -> p (i b)", i=TILES))
        nc.gpsimd.dma_start(out=bias[:], in_=bg.rearrange("(p t) -> p t", t=PACK))
        load_q(1)
        load_h(2)
        load_h(3)
        load_words("wk", wk_words)
        load_words("wq", wq_words)
        load_words("wv", wv_words)
        load_plane("wk", wk_scales, nc.sync)
        load_plane("wq", wq_scales, nc.sync)
        load_plane("wv", wv_scales, nc.sync)

        wg_sorted = keep.tile([P, PACK, P, 2], U8, name="wg_sorted", align_bytes=64)
        wg_plane_sorted = keep.tile([P, PACK, P], U8, name="wg_plane_sorted", align_bytes=64)
        q_wide, codes, planes = {}, {}, {}
        for name in ("h", "q", "p"):
            codes[name] = keep.tile([P, TOKENS], U32, name=name + "_mx_codes", align_bytes=64)
            planes[name] = keep.tile([P, TOKENS], U8, name=name + "_mx_plane", align_bytes=64)
        for j in range(PAIRS):
            q_wide[j] = keep.tile([P, 2, WIDTH], BF16, name="q_wide_%d" % j, align_bytes=64)
        grouped = {}
        for name in ("h", "q", "p"):
            for j in range(PAIRS):
                grouped[name, j] = keep.tile([P, 2 * WIDTH], BF16, name="%s_grouped_%d" % (name, j), align_bytes=64)
        scores = keep.tile([P, TILES, 2], F32, name="scores")
        gates = keep.tile([P, TILES, 2], F32, name="gates")
        state = {}
        banks_taken = []

        def next_bank(shape):
            banks_taken.append(1)
            return psum.tile(shape, F32, name="bank_%d" % (len(banks_taken) % 8))

        def sort_words():
            nc.vector.tensor_copy(out=wg_sorted[:], in_=weight_codes["wg"][:].rearrange("p (m t b) -> p t m b", t=PACK, b=2))

        def sort_plane():
            nc.vector.tensor_copy(out=wg_plane_sorted[:], in_=weight_plane["wg"][:].rearrange("p (m t) -> p t m", t=PACK))

        def widen(i):
            for b in range(4):
                first = (i % 4) * WIDTH + b * P
                target = q_wide[i // 2][:, i % 2, b * P : (b + 1) * P]
                source = q_raw[i // 4][:, first : first + P].bitcast(FP8)
                factor = q_factor[:, 4 * i + b : 4 * i + b + 1]
                if i in WIDEN_ON_VECTOR:
                    nc.vector.tensor_scalar(out=target, in0=source, scalar1=factor, scalar2=None, op0=ALU.mult)
                else:
                    nc.scalar.activation(out=target, in_=source, func=ACT.Copy, scale=factor)

        def turn(name, j):
            rows = h_sb[j] if name == "h" else q_wide[j]
            bank = next_bank([P, 4, P])
            for i in range(2):
                words = rows[:, i, :].bitcast(F32)
                for u in range(2):
                    nc.tensor.transpose(bank[:, 2 * i + u, :], words[:, u : 2 * P : 2], ident[:])
            state["turn", name, j] = bank

        def gather(name, j):
            nc.scalar.copy(
                out=grouped[name, j][:].bitcast(F32).rearrange("p (i r u) -> p i r u", i=2, u=2),
                in_=state["turn", name, j][:].rearrange("p (i u) r -> p i r u", u=2),
            )

        def quantise(name, j):
            cols = slice(2 * j * P, (2 * j + 2) * P)
            nc.vector.quantize_mx(
                out=codes[name][:, cols].bitcast(FP8X4), scales=planes[name][:, cols], in_=grouped[name, j][:]
            )

        def gate_matmul(i):
            bank = next_bank([P, PACK, P])
            cols = slice(i * P, (i + 1) * P)
            for t in range(PACK):
                nc.tensor.matmul_mx(
                    out=bank[:, t, :],
                    lhsT=wg_sorted[:, t, :, :].rearrange("p m b -> p (m b)").bitcast(FP4X4),
                    lhsT_scale=wg_plane_sorted[:, t, :],
                    rhs=codes["h"][:, cols].bitcast(FP8X4),
                    rhs_scale=planes["h"][:, cols],
                    start=True,
                    stop=True,
                )
            state["gate", i] = bank

        def add_bias(i):
            first = (i % 2) * WIDTH
            nc.vector.tensor_tensor(
                out=grouped["p", i // 2][:, first : first + WIDTH].rearrange("p (r t) -> p r t", t=PACK),
                in0=state["gate", i][:].rearrange("p t r -> p r t"),
                in1=bias[:].unsqueeze(1).to_broadcast([P, P, PACK]),
                op=ALU.add,
            )

        def project(weight, name, i):
            bank = next_bank([P, WIDTH])
            cols = slice(i * P, (i + 1) * P)
            nc.tensor.matmul_mx(
                out=bank[:],
                lhsT=codes[name][:, cols].bitcast(FP8X4),
                lhsT_scale=planes[name][:, cols],
                rhs=weight_codes[weight][:].bitcast(FP4X4),
                rhs_scale=weight_plane[weight][:],
                start=True,
                stop=True,
            )
            state[weight, name, i] = bank

        def copy_key(name, i):
            key_sb = keep.tile([P, WIDTH], F32, name="key_%s_%d" % (name, i))
            nc.scalar.copy(out=key_sb[:], in_=state["wk", name, i][:])
            state["key", name, i] = key_sb

        def score(name, i):
            side = 0 if name == "p" else 1
            key_sb = state["key", name, i]
            nc.vector.scalar_tensor_tensor(
                out=key_sb[:],
                in0=state["wq", name, i][:],
                scalar=1.0 / math.sqrt(WIDTH),
                in1=key_sb[:],
                op0=ALU.mult,
                op1=ALU.mult,
                accum_out=scores[:, i, side : side + 1],
            )

        def gate(i):
            for side in range(2):
                nc.scalar.activation(
                    out=gates[:, i, side : side + 1],
                    in_=scores[:, i, 1 - side : 2 - side],
                    func=ACT.Sigmoid,
                    scale=-1.0,
                    bias=scores[:, i, side : side + 1],
                )

        def weigh_p(i):
            z = keep.tile([P, WIDTH], F32, name="z_%d" % i)
            nc.scalar.activation(out=z[:], in_=state["wv", "p", i][:], func=ACT.Copy, scale=gates[:, i, 0:1])
            state["z", i] = z

        def weigh_q(i):
            y = keep.tile([P, WIDTH], F32, name="y_%d" % i)
            nc.scalar.activation(out=y[:], in_=state["wv", "q", i][:], func=ACT.Copy, scale=gates[:, i, 1:2])
            state["y", i] = y

        def mix(i):
            z = state["z", i]
            if i in MIX_ON_GPSIMD:
                nc.gpsimd.tensor_tensor(out=z[:], in0=z[:], in1=state["y", i][:], op=ALU.add)
            else:
                nc.vector.scalar_tensor_tensor(
                    out=z[:], in0=state["wv", "q", i][:], scalar=gates[:, i, 1:2], in1=z[:], op0=ALU.mult, op1=ALU.add
                )
            nc.sync.dma_start(out=out_rows[:, i, :], in_=z[:])

        stages = {
            "W": widen,
            "Th": lambda j: turn("h", j),
            "Tq": lambda j: turn("q", j),
            "Eh": lambda j: gather("h", j),
            "Eq": lambda j: gather("q", j),
            "Qh": lambda j: quantise("h", j),
            "Qq": lambda j: quantise("q", j),
            "Qp": lambda j: quantise("p", j),
            "P": gate_matmul,
            "Pe": add_bias,
            "Kp": lambda i: project("wk", "p", i),
            "Kq": lambda i: project("wk", "q", i),
            "Rp": lambda i: project("wq", "p", i),
            "Rq": lambda i: project("wq", "q", i),
            "Vp": lambda i: project("wv", "p", i),
            "Vq": lambda i: project("wv", "q", i),
            "Cp": lambda i: copy_key("p", i),
            "Cq": lambda i: copy_key("q", i),
            "Dp": lambda i: score("p", i),
            "Dq": lambda i: score("q", i),
            "G": gate,
            "Sv": weigh_p,
            "Y": weigh_q,
            "Z": mix,
            "perm": lambda i: sort_words() if i == 0 else sort_plane(),
        }
        for entry in ORDER:
            stages[entry[:-1]](int(entry[-1]))
